import numpy as np
import ml_dtypes


def mxq(x, axis, fmt="e4m3"):
    dtype, down = {"e4m3": (ml_dtypes.float8_e4m3fn, 7), "e5m2": (ml_dtypes.float8_e5m2, 14)}[fmt]
    v = np.moveaxis(np.asarray(x, np.float32).astype(ml_dtypes.bfloat16).astype(np.float64), axis, -1)
    blocks = v.reshape(v.shape[:-1] + (-1, 32))
    amax = np.abs(blocks).max(-1, keepdims=True)
    byte = np.maximum(np.where(amax > 0, np.frexp(amax)[1] - 1 + 127, 0) - down, 1)
    scale = np.exp2(byte - 127.0)
    codes = (blocks / scale).astype(np.float32).astype(dtype).astype(np.float64)
    return np.moveaxis((codes * scale).reshape(v.shape), -1, axis)


WIDE = False


def mx_kscale(k):
    if not WIDE:
        return np.ones(k)
    levels = np.array([10, -10, 5, -5, 0])
    if k % 512:
        return np.exp2(np.random.permutation(np.resize(levels, k // 32))).repeat(32)
    a = np.empty((k // 512, 16))
    for p in range(k // 512):
        a[p, :8] = np.random.permutation(np.resize(levels, 8))
        for g in range(8):
            far = levels[np.abs(levels - a[p, g]) >= 10]
            a[p, g + 8] = far[np.random.randint(len(far))]
    return np.exp2(a.ravel()).repeat(32)


def f64(x):
    return np.asarray(x).astype(np.float64)


def striped(idx):
    return np.tile(np.asarray(idx).reshape(-1, 16).T, (8, 1)).astype(np.uint16)


def unstriped(offs):
    return offs[:16].T.reshape(-1).astype(np.int64)


B, N, T, D, DV, NQ = 2, 512, 2048, 512, 512, 128
PAGE = 64


def setup_inputs():
    n = np.random.standard_normal
    pages = np.random.permutation(T // PAGE)[:B * N // PAGE]
    idx = (pages[:, None] * PAGE + np.arange(PAGE)[None, :]).reshape(-1)
    s = mx_kscale(D)[:, None]
    u = np.ones(T)
    u[idx] = mx_kscale(B * N)
    r = np.random.uniform(0.5, 2.0, T)
    k = n((D, T)) / s
    v = n((DV, T)) / (u * r)
    return {
        "qT": (n((B, D, NQ)) * s * (0.80 / np.sqrt(D))).astype(np.float32),
        "kT": k.astype(np.float32),
        "vT": v.astype(np.float32),
        "vs": np.tile(u * r, (128, 1)).astype(np.float32),
        "og": n((B, NQ, DV)).astype(np.float32),
        "offs": striped(idx),
    }


def reference(qT, kT, vT, vs, og, offs):
    idx = unstriped(offs)
    k = f64(kT)
    v = f64(vT)
    pick = lambda x: x[:, idx].reshape(x.shape[0], B, N).transpose(1, 0, 2)
    q = f64(qT)
    score = mxq(q, 1, "e4m3").transpose(0, 2, 1) @ mxq(pick(k), 1, "e4m3")
    m = score.max(-1, keepdims=True)
    p = np.exp(score - m)
    total = p.sum(-1, keepdims=True)
    w = p * pick(f64(vs))[:, :1, :]
    y = mxq(w, 2, "e4m3") @ mxq(pick(v).transpose(0, 2, 1), 1, "e4m3")
    y = y / total
    y = y / (1.0 + np.exp(-f64(og)))
    return y

@@ -1,0 +1,200 @@
+from contextlib import ExitStack
+
+import concourse.mybir as mybir
+from concourse.masks import make_identity
+
+B, N, T, D, DV, NQ = 2, 512, 2048, 512, 512, 128
+FLOPS = 2 * B * NQ * N * (D + DV)
+
+P = 128
+PACK = 4
+EB = DV // P
+
+F32 = mybir.dt.float32
+BF16 = mybir.dt.bfloat16
+U32 = mybir.dt.uint32
+U16 = mybir.dt.uint16
+U8 = mybir.dt.uint8
+FP8X4 = mybir.dt.float8_e4m3fn_x4
+ACT = mybir.ActivationFunctionType
+ALU = mybir.AluOpType
+AXIS = mybir.AxisListType
+
+
+def tile_attend_gate_kernel(tc, qT, kT, vT, vs, og, offs, out):
+    nc = tc.nc
+    with ExitStack() as ctx:
+        keep = ctx.enter_context(tc.tile_pool(name="keep", bufs=1))
+        psum = ctx.enter_context(tc.psum_pool(name="psum", bufs=1))
+
+        lists = keep.tile([P, B * N // 16], U16, name="lists")
+        nc.sync.dma_start(lists[:], offs)
+        q_raw = keep.tile([P, B, PACK, NQ], F32, name="q_raw")
+        nc.sync.dma_start(q_raw[:], qT.rearrange("b (p j) q -> p b j q", j=PACK))
+
+        scale_pool = keep.tile([P, T], F32, name="scale_pool")
+        nc.vector.memset(scale_pool[:], 0.0)
+        nc.scalar.dma_start(scale_pool[0:1, :], vs[0:1, :])
+
+        k_rows = kT.rearrange("(p j) t -> p j t", j=PACK)
+        k_pool = []
+        for j in range(PACK):
+            k_plane = keep.tile([P, T], F32, name=f"k_pool{j}")
+            nc.sync.dma_start(k_plane[:], k_rows[:, j, :])
+            k_pool.append(k_plane)
+        v_pool = []
+        for e in range(EB):
+            v_plane = keep.tile([P, T], F32, name=f"v_pool{e}")
+            nc.sync.dma_start(v_plane[:], vT[e * P : (e + 1) * P, :])
+            v_pool.append(v_plane)
+        gate = keep.tile([P, B, DV], F32, name="gate")
+        nc.sync.dma_start(gate[:], og.rearrange("b q e -> q b e"))
+
+        warm = keep.tile([P, 1], F32, name="warm")
+        nc.vector.memset(warm[:], 0.0)
+        nc.scalar.activation(warm[:], warm[:], ACT.Exp)
+        ident_f = keep.tile([P, P], F32, name="ident_f")
+        make_identity(nc, ident_f[:])
+        ident_b = keep.tile([P, P], BF16, name="ident_b")
+        make_identity(nc, ident_b[:])
+
+        q_bf = keep.tile([P, B, NQ, PACK], BF16, align_bytes=64, name="q_bf")
+        q_codes = keep.tile([P, B * NQ], U32, align_bytes=64, name="q_codes")
+        q_scales = keep.tile([P, B * NQ], U8, align_bytes=64, name="q_scales")
+        nc.scalar.copy(q_bf[:], q_raw[:].rearrange("p b j q -> p b q j"))
+        nc.vector.quantize_mx(
+            out=q_codes[:].bitcast(FP8X4), scales=q_scales[:], in_=q_bf[:].rearrange("p b q j -> p (b q j)")
+        )
+
+        vs_row = keep.tile([P, B * N], F32, name="vs_row")
+        nc.vector.tensor_copy(vs_row[:], scale_pool[:].indirect(lists[:]))
+        vs_col = []
+        for b in range(B):
+            turned = psum.tile([P, PACK, P], F32, tag="wide", bufs=3, name="turned")
+            for t in range(PACK):
+                nc.tensor.transpose(turned[:, t, :], vs_row[:, b * N + t : (b + 1) * N : PACK], ident_f[:])
+            col = keep.tile([P, PACK], F32, name=f"vs_col{b}")
+            nc.scalar.copy(col[:], turned[:, :, 0])
+            vs_col.append(col)
+
+        k_got = keep.tile([P, PACK, B * N], F32, name="k_got")
+        k_bf = keep.tile([P, B * N, PACK], BF16, align_bytes=64, name="k_bf")
+        k_codes = keep.tile([P, B * N], U32, align_bytes=64, name="k_codes")
+        k_scales = keep.tile([P, B * N], U8, align_bytes=64, name="k_scales")
+        for j in range(PACK):
+            if j < PACK - 1:
+                nc.vector.tensor_copy(k_got[:, j, :], k_pool[j][:].indirect(lists[:]))
+            else:
+                for b in range(B):
+                    nc.vector.tensor_copy(
+                        k_got[:, j, b * N : (b + 1) * N],
+                        k_pool[j][:].indirect(lists[:, b * N // 16 : (b + 1) * N // 16]),
+                    )
+        for b in range(B):
+            s = slice(b * N, (b + 1) * N)
+            dst = k_bf[:, s, :].rearrange("p (c i) t -> p c t i", i=4)
+            got = k_got[:, :, s].rearrange("p t (c i) -> p c t i", i=4)
+            if b == 0:
+                nc.scalar.copy(dst, got)
+            else:
+                nc.vector.tensor_copy(dst, got)
+        for b in (1, 0):
+            s = slice(b * N, (b + 1) * N)
+            nc.vector.quantize_mx(
+                out=k_codes[:, s].bitcast(FP8X4), scales=k_scales[:, s], in_=k_bf[:, s, :].rearrange("p n t -> p (n t)")
+            )
+
+        top = keep.tile([P, B], F32, name="top")
+        minus = [keep.tile([P, 1], F32, name=f"minus{b}") for b in range(B)]
+        total = [keep.tile([P, 1], F32, name=f"total{b}") for b in range(B)]
+        half = [keep.tile([P, 1], F32, name=f"half{b}") for b in range(B)]
+        weight = [keep.tile([P, PACK, P], F32, name=f"weight{b}") for b in range(B)]
+        w_bf = [keep.tile([P, NQ, PACK], BF16, align_bytes=64, name=f"w_bf{b}") for b in range(B)]
+        w_codes = [keep.tile([P, NQ], U32, align_bytes=64, name=f"w_codes{b}") for b in range(B)]
+        w_scales = [keep.tile([P, NQ], U8, align_bytes=64, name=f"w_scales{b}") for b in range(B)]
+        for b in (1, 0):
+            s = slice(b * N, (b + 1) * N)
+            qs = slice(b * NQ, (b + 1) * NQ)
+            score = psum.tile([P, N], F32, tag="wide", bufs=3, name="score")
+            nc.tensor.matmul_mx(
+                out=score[:],
+                lhsT=q_codes[:, qs].bitcast(FP8X4),
+                lhsT_scale=q_scales[:, qs],
+                rhs=k_codes[:, s].bitcast(FP8X4),
+                rhs_scale=k_scales[:, s],
+                start=True,
+                stop=True,
+            )
+            nc.vector.reduce_max(minus[b][:], score[:], axis=AXIS.X)
+            nc.scalar.mul(top[:, b : b + 1], minus[b][:], -1.0)
+            nc.scalar.activation(
+                weight[b][:],
+                score[:].rearrange("p (c t) -> p t c", t=PACK),
+                ACT.Exp,
+                bias=top[:, b : b + 1],
+                accum_out=total[b][:],
+            )
+            turned = psum.tile([P, PACK, P], F32, tag="wide", bufs=3, name="turned")
+            for t in range(PACK):
+                nc.tensor.transpose(turned[:, t, :], weight[b][:, t, :], ident_f[:])
+            nc.vector.tensor_tensor(
+                w_bf[b][:],
+                turned[:].rearrange("p t q -> p q t"),
+                vs_col[b][:].unsqueeze(1).to_broadcast([P, NQ, PACK]),
+                ALU.mult,
+            )
+            nc.vector.quantize_mx(
+                out=w_codes[b][:].bitcast(FP8X4), scales=w_scales[b][:], in_=w_bf[b][:].rearrange("p q t -> p (q t)")
+            )
+            nc.vector.reciprocal(half[b][:], total[b][:])
+            nc.vector.tensor_scalar_mul(half[b][:], half[b][:], 0.5)
+
+        v_codes = []
+        v_scales = []
+        for e in range(EB):
+            v_bf = keep.tile([P, B, P, PACK], BF16, align_bytes=64, name=f"v_bf{e}")
+            codes = keep.tile([P, B * P], U32, align_bytes=64, name=f"v_codes{e}")
+            scales = keep.tile([P, B * P], U8, align_bytes=64, name=f"v_scales{e}")
+            v_codes.append(codes)
+            v_scales.append(scales)
+            for b in range(B):
+                v_got = keep.tile([P, PACK, P], BF16, name=f"v_got{e}{b}")
+                nc.vector.tensor_copy(
+                    v_got[:].rearrange("p t c -> p c t"),
+                    v_pool[e][:].indirect(lists[:, b * N // 16 : (b + 1) * N // 16]),
+                )
+                turned_v = psum.tile([P, PACK, P], BF16, tag="values", bufs=3, name="turned_v")
+                for t in range(PACK):
+                    nc.tensor.transpose(turned_v[:, t, :], v_got[:, t, :], ident_b[:])
+                nc.scalar.copy(v_bf[:, b, :, :], turned_v[:].rearrange("p t e -> p e t"))
+                cols = slice(b * P, (b + 1) * P)
+                nc.vector.quantize_mx(
+                    out=codes[:, cols].bitcast(FP8X4),
+                    scales=scales[:, cols],
+                    in_=v_bf[:, b, :, :].rearrange("p e t -> p (e t)"),
+                )
+
+        tanh = keep.tile([P, B, DV], F32, name="tanh")
+        factor = keep.tile([P, B, DV], F32, name="factor")
+        for b in range(B):
+            nc.scalar.activation(tanh[:, b, :], gate[:, b, :], ACT.Tanh, scale=0.5)
+            nc.vector.tensor_scalar(factor[:, b, :], tanh[:, b, :], 1.0, half[b][:], ALU.add, ALU.mult)
+
+        out_rows = out.rearrange("b q e -> q b e")
+        for e in range(EB):
+            y = psum.tile([P, B, P], F32, tag="y", bufs=2, name="y")
+            es = slice(e * P, (e + 1) * P)
+            for b in range(B):
+                cols = slice(b * P, (b + 1) * P)
+                nc.tensor.matmul_mx(
+                    out=y[:, b, :],
+                    lhsT=w_codes[b][:].bitcast(FP8X4),
+                    lhsT_scale=w_scales[b][:],
+                    rhs=v_codes[e][:, cols].bitcast(FP8X4),
+                    rhs_scale=v_scales[e][:, cols],
+                    start=True,
+                    stop=True,
+                )
+            res = keep.tile([P, B, P], F32, name=f"res{e}")
+            nc.vector.tensor_tensor(res[:], y[:], factor[:, :, es], ALU.mult)
+            nc.sync.dma_start(out_rows[:, :, es], res[:])

@@ -29,42 +29,32 @@ def tile_attend_gate_kernel(tc, qT, kT, vT, vs, og, offs, out):
 
         lists = keep.tile([P, B * N // 16], U16, name="lists")
         nc.sync.dma_start(lists[:], offs)
-        q_raw = keep.tile([P, B, PACK, NQ], F32, name="q_raw")
-        nc.sync.dma_start(q_raw[:], qT.rearrange("b (p j) q -> p b j q", j=PACK))
-
+        k_rows = kT.rearrange("(p j) t -> p j t", j=PACK)
+        k_pool = [keep.tile([P, T], F32, name=f"k_pool{j}") for j in range(PACK)]
+        v_pool = [keep.tile([P, T], F32, name=f"v_pool{e}") for e in range(EB)]
         scale_pool = keep.tile([P, T], F32, name="scale_pool")
         nc.vector.memset(scale_pool[:], 0.0)
-        nc.scalar.dma_start(scale_pool[0:1, :], vs[0:1, :])
-
-        k_rows = kT.rearrange("(p j) t -> p j t", j=PACK)
-        k_pool = []
-        for j in range(PACK):
-            k_plane = keep.tile([P, T], F32, name=f"k_pool{j}")
-            nc.sync.dma_start(k_plane[:], k_rows[:, j, :])
-            k_pool.append(k_plane)
-        v_pool = []
+        nc.sync.dma_start(k_pool[0][:], k_rows[:, 0, :])
+        nc.sync.dma_start(scale_pool[0:1, :], vs[0:1, :])
+        for j in range(1, PACK):
+            nc.sync.dma_start(k_pool[j][:], k_rows[:, j, :])
+        q_raw = keep.tile([P, B, PACK, NQ], F32, name="q_raw")
+        nc.sync.dma_start(q_raw[:], qT.rearrange("b (p j) q -> p b j q", j=PACK))
+        gates = [keep.tile([P, B, DV // 2], F32, name=f"gate{h}") for h in range(2)]
+        gate_rows = og.rearrange("b q e -> q b e")
         for e in range(EB):
-            v_plane = keep.tile([P, T], F32, name=f"v_pool{e}")
-            nc.sync.dma_start(v_plane[:], vT[e * P : (e + 1) * P, :])
-            v_pool.append(v_plane)
-        gate = keep.tile([P, B, DV], F32, name="gate")
-        nc.sync.dma_start(gate[:], og.rearrange("b q e -> q b e"))
+            if e == EB - 1:
+                nc.sync.dma_start(gates[0][:], gate_rows[:, :, : DV // 2])
+            nc.sync.dma_start(v_pool[e][:], vT[e * P : (e + 1) * P, :])
+        nc.sync.dma_start(gates[1][:], gate_rows[:, :, DV // 2 :])
 
         warm = keep.tile([P, 1], F32, name="warm")
-        nc.vector.memset(warm[:], 0.0)
+        nc.gpsimd.memset(warm[:], 0.0)
         nc.scalar.activation(warm[:], warm[:], ACT.Exp)
         ident_f = keep.tile([P, P], F32, name="ident_f")
         make_identity(nc, ident_f[:])
         ident_b = keep.tile([P, P], BF16, name="ident_b")
         make_identity(nc, ident_b[:])
-
-        q_bf = keep.tile([P, B, NQ, PACK], BF16, align_bytes=64, name="q_bf")
-        q_codes = keep.tile([P, B * NQ], U32, align_bytes=64, name="q_codes")
-        q_scales = keep.tile([P, B * NQ], U8, align_bytes=64, name="q_scales")
-        nc.scalar.copy(q_bf[:], q_raw[:].rearrange("p b j q -> p b q j"))
-        nc.vector.quantize_mx(
-            out=q_codes[:].bitcast(FP8X4), scales=q_scales[:], in_=q_bf[:].rearrange("p b q j -> p (b q j)")
-        )
 
         vs_row = keep.tile([P, B * N], F32, name="vs_row")
         nc.vector.tensor_copy(vs_row[:], scale_pool[:].indirect(lists[:]))
@@ -90,21 +80,26 @@ def tile_attend_gate_kernel(tc, qT, kT, vT, vs, og, offs, out):
                         k_got[:, j, b * N : (b + 1) * N],
                         k_pool[j][:].indirect(lists[:, b * N // 16 : (b + 1) * N // 16]),
                     )
-        for b in range(B):
-            s = slice(b * N, (b + 1) * N)
-            dst = k_bf[:, s, :].rearrange("p (c i) t -> p c t i", i=4)
-            got = k_got[:, :, s].rearrange("p t (c i) -> p c t i", i=4)
-            if b == 0:
-                nc.scalar.copy(dst, got)
-            else:
-                nc.vector.tensor_copy(dst, got)
-        for b in (1, 0):
-            s = slice(b * N, (b + 1) * N)
-            nc.vector.quantize_mx(
-                out=k_codes[:, s].bitcast(FP8X4), scales=k_scales[:, s], in_=k_bf[:, s, :].rearrange("p n t -> p (n t)")
+
+        def interleave_keys(copy, first, last):
+            copy(
+                k_bf[:, first:last, :].rearrange("p (c i) t -> p c t i", i=4),
+                k_got[:, :, first:last].rearrange("p t (c i) -> p c t i", i=4),
             )
 
-        top = keep.tile([P, B], F32, name="top")
+        for b in range(B):
+            interleave_keys(nc.scalar.copy, b * N, b * N + N // 2)
+            interleave_keys(nc.vector.tensor_copy, b * N + N // 2, (b + 1) * N)
+
+        q_bf = keep.tile([P, B, NQ, PACK], BF16, align_bytes=64, name="q_bf")
+        q_codes = keep.tile([P, B * NQ], U32, align_bytes=64, name="q_codes")
+        q_scales = keep.tile([P, B * NQ], U8, align_bytes=64, name="q_scales")
+        nc.vector.tensor_copy(q_bf[:], q_raw[:].rearrange("p b j q -> p b q j"))
+        nc.vector.quantize_mx(
+            out=q_codes[:].bitcast(FP8X4), scales=q_scales[:], in_=q_bf[:].rearrange("p b q j -> p (b q j)")
+        )
+
+        top = [keep.tile([P, 1], F32, name=f"top{b}") for b in range(B)]
         minus = [keep.tile([P, 1], F32, name=f"minus{b}") for b in range(B)]
         total = [keep.tile([P, 1], F32, name=f"total{b}") for b in range(B)]
         half = [keep.tile([P, 1], F32, name=f"half{b}") for b in range(B)]
@@ -112,9 +107,13 @@ def tile_attend_gate_kernel(tc, qT, kT, vT, vs, og, offs, out):
         w_bf = [keep.tile([P, NQ, PACK], BF16, align_bytes=64, name=f"w_bf{b}") for b in range(B)]
         w_codes = [keep.tile([P, NQ], U32, align_bytes=64, name=f"w_codes{b}") for b in range(B)]
         w_scales = [keep.tile([P, NQ], U8, align_bytes=64, name=f"w_scales{b}") for b in range(B)]
-        for b in (1, 0):
+
+        def scores(b):
             s = slice(b * N, (b + 1) * N)
             qs = slice(b * NQ, (b + 1) * NQ)
+            nc.vector.quantize_mx(
+                out=k_codes[:, s].bitcast(FP8X4), scales=k_scales[:, s], in_=k_bf[:, s, :].rearrange("p n t -> p (n t)")
+            )
             score = psum.tile([P, N], F32, tag="wide", bufs=3, name="score")
             nc.tensor.matmul_mx(
                 out=score[:],
@@ -125,15 +124,20 @@ def tile_attend_gate_kernel(tc, qT, kT, vT, vs, og, offs, out):
                 start=True,
                 stop=True,
             )
-            nc.vector.reduce_max(minus[b][:], score[:], axis=AXIS.X)
-            nc.scalar.mul(top[:, b : b + 1], minus[b][:], -1.0)
+            return score
+
+        def softmax(b, score):
+            nc.vector.reduce_max(top[b][:], score[:], axis=AXIS.X)
+            nc.scalar.mul(minus[b][:], top[b][:], -1.0)
             nc.scalar.activation(
                 weight[b][:],
                 score[:].rearrange("p (c t) -> p t c", t=PACK),
                 ACT.Exp,
-                bias=top[:, b : b + 1],
+                bias=minus[b][:],
                 accum_out=total[b][:],
             )
+
+        def weights(b):
             turned = psum.tile([P, PACK, P], F32, tag="wide", bufs=3, name="turned")
             for t in range(PACK):
                 nc.tensor.transpose(turned[:, t, :], weight[b][:, t, :], ident_f[:])
@@ -149,39 +153,47 @@ def tile_attend_gate_kernel(tc, qT, kT, vT, vs, og, offs, out):
             nc.vector.reciprocal(half[b][:], total[b][:])
             nc.vector.tensor_scalar_mul(half[b][:], half[b][:], 0.5)
 
-        v_codes = []
-        v_scales = []
-        for e in range(EB):
-            v_bf = keep.tile([P, B, P, PACK], BF16, align_bytes=64, name=f"v_bf{e}")
-            codes = keep.tile([P, B * P], U32, align_bytes=64, name=f"v_codes{e}")
-            scales = keep.tile([P, B * P], U8, align_bytes=64, name=f"v_scales{e}")
-            v_codes.append(codes)
-            v_scales.append(scales)
+        v_got = [keep.tile([P, B, PACK, P], BF16, name=f"v_got{e}") for e in range(EB)]
+        v_bf = [keep.tile([P, B, P, PACK], BF16, align_bytes=64, name=f"v_bf{e}") for e in range(EB)]
+        v_codes = [keep.tile([P, B * P], U32, align_bytes=64, name=f"v_codes{e}") for e in range(EB)]
+        v_scales = [keep.tile([P, B * P], U8, align_bytes=64, name=f"v_scales{e}") for e in range(EB)]
+
+        def gather_values(e, split):
+            if split:
+                for b in range(B):
+                    nc.vector.tensor_copy(
+                        v_got[e][:, b, :, :].rearrange("p t c -> p c t"),
+                        v_pool[e][:].indirect(lists[:, b * N // 16 : (b + 1) * N // 16]),
+                    )
+            else:
+                nc.vector.tensor_copy(v_got[e][:].rearrange("p b t c -> p b c t"), v_pool[e][:].indirect(lists[:]))
             for b in range(B):
-                v_got = keep.tile([P, PACK, P], BF16, name=f"v_got{e}{b}")
-                nc.vector.tensor_copy(
-                    v_got[:].rearrange("p t c -> p c t"),
-                    v_pool[e][:].indirect(lists[:, b * N // 16 : (b + 1) * N // 16]),
-                )
                 turned_v = psum.tile([P, PACK, P], BF16, tag="values", bufs=3, name="turned_v")
                 for t in range(PACK):
-                    nc.tensor.transpose(turned_v[:, t, :], v_got[:, t, :], ident_b[:])
-                nc.scalar.copy(v_bf[:, b, :, :], turned_v[:].rearrange("p t e -> p e t"))
-                cols = slice(b * P, (b + 1) * P)
-                nc.vector.quantize_mx(
-                    out=codes[:, cols].bitcast(FP8X4),
-                    scales=scales[:, cols],
-                    in_=v_bf[:, b, :, :].rearrange("p e t -> p (e t)"),
+                    nc.tensor.transpose(turned_v[:, t, :], v_got[e][:, b, t, :], ident_b[:])
+                nc.scalar.copy(v_bf[e][:, b, :, :], turned_v[:].rearrange("p t e -> p e t"))
+
+        def quantize_values(e, first, last):
+            cols = slice(first * P, last * P)
+            nc.vector.quantize_mx(
+                out=v_codes[e][:, cols].bitcast(FP8X4),
+                scales=v_scales[e][:, cols],
+                in_=v_bf[e][:, first:last, :, :].rearrange("p b e t -> p (b e t)"),
+            )
+
+        tanh = [keep.tile([P, B, DV // 2], F32, name=f"tanh{h}") for h in range(2)]
+        factor = keep.tile([P, B, DV], F32, name="factor")
+
+        def gate_factor(h):
+            nc.scalar.activation(tanh[h][:], gates[h][:], ACT.Tanh, scale=0.5)
+            for b in range(B):
+                nc.vector.tensor_scalar(
+                    factor[:, b, h * (DV // 2) : (h + 1) * (DV // 2)], tanh[h][:, b, :], 1.0, half[b][:], ALU.add, ALU.mult
                 )
 
-        tanh = keep.tile([P, B, DV], F32, name="tanh")
-        factor = keep.tile([P, B, DV], F32, name="factor")
-        for b in range(B):
-            nc.scalar.activation(tanh[:, b, :], gate[:, b, :], ACT.Tanh, scale=0.5)
-            nc.vector.tensor_scalar(factor[:, b, :], tanh[:, b, :], 1.0, half[b][:], ALU.add, ALU.mult)
+        res = keep.tile([P, B, DV], F32, name="res")
 
-        out_rows = out.rearrange("b q e -> q b e")
-        for e in range(EB):
+        def attend(e):
             y = psum.tile([P, B, P], F32, tag="y", bufs=2, name="y")
             es = slice(e * P, (e + 1) * P)
             for b in range(B):
@@ -195,6 +207,35 @@ def tile_attend_gate_kernel(tc, qT, kT, vT, vs, og, offs, out):
                     start=True,
                     stop=True,
                 )
-            res = keep.tile([P, B, P], F32, name=f"res{e}")
-            nc.vector.tensor_tensor(res[:], y[:], factor[:, :, es], ALU.mult)
-            nc.sync.dma_start(out_rows[:, :, es], res[:])
+            nc.vector.tensor_tensor(res[:, :, es], y[:], factor[:, :, es], ALU.mult)
+
+        out_rows = out.rearrange("b q e -> q b e")
+
+        def store(first, last):
+            es = slice(first * P, last * P)
+            nc.sync.dma_start(out_rows[:, :, es], res[:, :, es])
+
+        score0 = scores(0)
+        score1 = scores(1)
+        softmax(0, score0)
+        gather_values(0, False)
+        softmax(1, score1)
+        weights(0)
+        gather_values(1, False)
+        weights(1)
+        quantize_values(0, 0, 2)
+        gather_values(2, False)
+        quantize_values(1, 0, 2)
+        gate_factor(0)
+        attend(0)
+        attend(1)
+        store(0, 2)
+        quantize_values(2, 0, 2)
+        gather_values(3, True)
+        gate_factor(1)
+        attend(2)
+        store(2, 3)
+        quantize_values(3, 0, 1)
+        quantize_values(3, 1, 2)
+        attend(3)
+        store(3, 4)

from contextlib import ExitStack

import concourse.mybir as mybir
from concourse.masks import make_identity

B, N, T, D, DV, NQ = 2, 512, 2048, 512, 512, 128
FLOPS = 2 * B * NQ * N * (D + DV)

P = 128
PACK = 4
EB = DV // P

F32 = mybir.dt.float32
BF16 = mybir.dt.bfloat16
U32 = mybir.dt.uint32
U16 = mybir.dt.uint16
U8 = mybir.dt.uint8
FP8X4 = mybir.dt.float8_e4m3fn_x4
ACT = mybir.ActivationFunctionType
ALU = mybir.AluOpType
AXIS = mybir.AxisListType


def tile_attend_gate_kernel(tc, qT, kT, vT, vs, og, offs, out):
    nc = tc.nc
    with ExitStack() as ctx:
        keep = ctx.enter_context(tc.tile_pool(name="keep", bufs=1))
        psum = ctx.enter_context(tc.psum_pool(name="psum", bufs=1))

        lists = keep.tile([P, B * N // 16], U16, name="lists")
        nc.sync.dma_start(lists[:], offs)
        k_rows = kT.rearrange("(p j) t -> p j t", j=PACK)
        k_pool = [keep.tile([P, T], F32, name=f"k_pool{j}") for j in range(PACK)]
        v_pool = [keep.tile([P, T], F32, name=f"v_pool{e}") for e in range(EB)]
        scale_pool = keep.tile([P, T], F32, name="scale_pool")
        nc.vector.memset(scale_pool[:], 0.0)
        nc.sync.dma_start(k_pool[0][:], k_rows[:, 0, :])
        nc.sync.dma_start(scale_pool[0:1, :], vs[0:1, :])
        for j in range(1, PACK):
            nc.sync.dma_start(k_pool[j][:], k_rows[:, j, :])
        q_raw = keep.tile([P, B, PACK, NQ], F32, name="q_raw")
        nc.sync.dma_start(q_raw[:], qT.rearrange("b (p j) q -> p b j q", j=PACK))
        gates = [keep.tile([P, B, DV // 2], F32, name=f"gate{h}") for h in range(2)]
        gate_rows = og.rearrange("b q e -> q b e")
        for e in range(EB):
            if e == EB - 1:
                nc.sync.dma_start(gates[0][:], gate_rows[:, :, : DV // 2])
            nc.sync.dma_start(v_pool[e][:], vT[e * P : (e + 1) * P, :])
        nc.sync.dma_start(gates[1][:], gate_rows[:, :, DV // 2 :])

        warm = keep.tile([P, 1], F32, name="warm")
        nc.gpsimd.memset(warm[:], 0.0)
        nc.scalar.activation(warm[:], warm[:], ACT.Exp)
        ident_f = keep.tile([P, P], F32, name="ident_f")
        make_identity(nc, ident_f[:])
        ident_b = keep.tile([P, P], BF16, name="ident_b")
        make_identity(nc, ident_b[:])

        vs_row = keep.tile([P, B * N], F32, name="vs_row")
        nc.vector.tensor_copy(vs_row[:], scale_pool[:].indirect(lists[:]))
        vs_col = []
        for b in range(B):
            turned = psum.tile([P, PACK, P], F32, tag="wide", bufs=3, name="turned")
            for t in range(PACK):
                nc.tensor.transpose(turned[:, t, :], vs_row[:, b * N + t : (b + 1) * N : PACK], ident_f[:])
            col = keep.tile([P, PACK], F32, name=f"vs_col{b}")
            nc.scalar.copy(col[:], turned[:, :, 0])
            vs_col.append(col)

        k_got = keep.tile([P, PACK, B * N], F32, name="k_got")
        k_bf = keep.tile([P, B * N, PACK], BF16, align_bytes=64, name="k_bf")
        k_codes = keep.tile([P, B * N], U32, align_bytes=64, name="k_codes")
        k_scales = keep.tile([P, B * N], U8, align_bytes=64, name="k_scales")
        for j in range(PACK):
            if j < PACK - 1:
                nc.vector.tensor_copy(k_got[:, j, :], k_pool[j][:].indirect(lists[:]))
            else:
                for b in range(B):
                    nc.vector.tensor_copy(
                        k_got[:, j, b * N : (b + 1) * N],
                        k_pool[j][:].indirect(lists[:, b * N // 16 : (b + 1) * N // 16]),
                    )

        def interleave_keys(copy, first, last):
            copy(
                k_bf[:, first:last, :].rearrange("p (c i) t -> p c t i", i=4),
                k_got[:, :, first:last].rearrange("p t (c i) -> p c t i", i=4),
            )

        for b in range(B):
            interleave_keys(nc.scalar.copy, b * N, b * N + N // 2)
            interleave_keys(nc.vector.tensor_copy, b * N + N // 2, (b + 1) * N)

        q_bf = keep.tile([P, B, NQ, PACK], BF16, align_bytes=64, name="q_bf")
        q_codes = keep.tile([P, B * NQ], U32, align_bytes=64, name="q_codes")
        q_scales = keep.tile([P, B * NQ], U8, align_bytes=64, name="q_scales")
        nc.vector.tensor_copy(q_bf[:], q_raw[:].rearrange("p b j q -> p b q j"))
        nc.vector.quantize_mx(
            out=q_codes[:].bitcast(FP8X4), scales=q_scales[:], in_=q_bf[:].rearrange("p b q j -> p (b q j)")
        )

        top = [keep.tile([P, 1], F32, name=f"top{b}") for b in range(B)]
        minus = [keep.tile([P, 1], F32, name=f"minus{b}") for b in range(B)]
        total = [keep.tile([P, 1], F32, name=f"total{b}") for b in range(B)]
        half = [keep.tile([P, 1], F32, name=f"half{b}") for b in range(B)]
        weight = [keep.tile([P, PACK, P], F32, name=f"weight{b}") for b in range(B)]
        w_bf = [keep.tile([P, NQ, PACK], BF16, align_bytes=64, name=f"w_bf{b}") for b in range(B)]
        w_codes = [keep.tile([P, NQ], U32, align_bytes=64, name=f"w_codes{b}") for b in range(B)]
        w_scales = [keep.tile([P, NQ], U8, align_bytes=64, name=f"w_scales{b}") for b in range(B)]

        def scores(b):
            s = slice(b * N, (b + 1) * N)
            qs = slice(b * NQ, (b + 1) * NQ)
            nc.vector.quantize_mx(
                out=k_codes[:, s].bitcast(FP8X4), scales=k_scales[:, s], in_=k_bf[:, s, :].rearrange("p n t -> p (n t)")
            )
            score = psum.tile([P, N], F32, tag="wide", bufs=3, name="score")
            nc.tensor.matmul_mx(
                out=score[:],
                lhsT=q_codes[:, qs].bitcast(FP8X4),
                lhsT_scale=q_scales[:, qs],
                rhs=k_codes[:, s].bitcast(FP8X4),
                rhs_scale=k_scales[:, s],
                start=True,
                stop=True,
            )
            return score

        def softmax(b, score):
            nc.vector.reduce_max(top[b][:], score[:], axis=AXIS.X)
            nc.scalar.mul(minus[b][:], top[b][:], -1.0)
            nc.scalar.activation(
                weight[b][:],
                score[:].rearrange("p (c t) -> p t c", t=PACK),
                ACT.Exp,
                bias=minus[b][:],
                accum_out=total[b][:],
            )

        def weights(b):
            turned = psum.tile([P, PACK, P], F32, tag="wide", bufs=3, name="turned")
            for t in range(PACK):
                nc.tensor.transpose(turned[:, t, :], weight[b][:, t, :], ident_f[:])
            nc.vector.tensor_tensor(
                w_bf[b][:],
                turned[:].rearrange("p t q -> p q t"),
                vs_col[b][:].unsqueeze(1).to_broadcast([P, NQ, PACK]),
                ALU.mult,
            )
            nc.vector.quantize_mx(
                out=w_codes[b][:].bitcast(FP8X4), scales=w_scales[b][:], in_=w_bf[b][:].rearrange("p q t -> p (q t)")
            )
            nc.vector.reciprocal(half[b][:], total[b][:])
            nc.vector.tensor_scalar_mul(half[b][:], half[b][:], 0.5)

        v_got = [keep.tile([P, B, PACK, P], BF16, name=f"v_got{e}") for e in range(EB)]
        v_bf = [keep.tile([P, B, P, PACK], BF16, align_bytes=64, name=f"v_bf{e}") for e in range(EB)]
        v_codes = [keep.tile([P, B * P], U32, align_bytes=64, name=f"v_codes{e}") for e in range(EB)]
        v_scales = [keep.tile([P, B * P], U8, align_bytes=64, name=f"v_scales{e}") for e in range(EB)]

        def gather_values(e, split):
            if split:
                for b in range(B):
                    nc.vector.tensor_copy(
                        v_got[e][:, b, :, :].rearrange("p t c -> p c t"),
                        v_pool[e][:].indirect(lists[:, b * N // 16 : (b + 1) * N // 16]),
                    )
            else:
                nc.vector.tensor_copy(v_got[e][:].rearrange("p b t c -> p b c t"), v_pool[e][:].indirect(lists[:]))
            for b in range(B):
                turned_v = psum.tile([P, PACK, P], BF16, tag="values", bufs=3, name="turned_v")
                for t in range(PACK):
                    nc.tensor.transpose(turned_v[:, t, :], v_got[e][:, b, t, :], ident_b[:])
                nc.scalar.copy(v_bf[e][:, b, :, :], turned_v[:].rearrange("p t e -> p e t"))

        def quantize_values(e, first, last):
            cols = slice(first * P, last * P)
            nc.vector.quantize_mx(
                out=v_codes[e][:, cols].bitcast(FP8X4),
                scales=v_scales[e][:, cols],
                in_=v_bf[e][:, first:last, :, :].rearrange("p b e t -> p (b e t)"),
            )

        tanh = [keep.tile([P, B, DV // 2], F32, name=f"tanh{h}") for h in range(2)]
        factor = keep.tile([P, B, DV], F32, name="factor")

        def gate_factor(h):
            nc.scalar.activation(tanh[h][:], gates[h][:], ACT.Tanh, scale=0.5)
            for b in range(B):
                nc.vector.tensor_scalar(
                    factor[:, b, h * (DV // 2) : (h + 1) * (DV // 2)], tanh[h][:, b, :], 1.0, half[b][:], ALU.add, ALU.mult
                )

        res = keep.tile([P, B, DV], F32, name="res")

        def attend(e):
            y = psum.tile([P, B, P], F32, tag="y", bufs=2, name="y")
            es = slice(e * P, (e + 1) * P)
            for b in range(B):
                cols = slice(b * P, (b + 1) * P)
                nc.tensor.matmul_mx(
                    out=y[:, b, :],
                    lhsT=w_codes[b][:].bitcast(FP8X4),
                    lhsT_scale=w_scales[b][:],
                    rhs=v_codes[e][:, cols].bitcast(FP8X4),
                    rhs_scale=v_scales[e][:, cols],
                    start=True,
                    stop=True,
                )
            nc.vector.tensor_tensor(res[:, :, es], y[:], factor[:, :, es], ALU.mult)

        out_rows = out.rearrange("b q e -> q b e")

        def store(first, last):
            es = slice(first * P, last * P)
            nc.sync.dma_start(out_rows[:, :, es], res[:, :, es])

        score0 = scores(0)
        score1 = scores(1)
        softmax(0, score0)
        gather_values(0, False)
        softmax(1, score1)
        weights(0)
        gather_values(1, False)
        weights(1)
        quantize_values(0, 0, 2)
        gather_values(2, False)
        quantize_values(1, 0, 2)
        gate_factor(0)
        attend(0)
        attend(1)
        store(0, 2)
        quantize_values(2, 0, 2)
        gather_values(3, True)
        gate_factor(1)
        attend(2)
        store(2, 3)
        quantize_values(3, 0, 1)
        quantize_values(3, 1, 2)
        attend(3)
        store(3, 4)
